import numpy as np
import ml_dtypes


def mxq(x, axis, fmt="e4m3"):
    dtype, down = {"e4m3": (ml_dtypes.float8_e4m3fn, 7), "e5m2": (ml_dtypes.float8_e5m2, 14)}[fmt]
    v = np.moveaxis(np.asarray(x, np.float32).astype(ml_dtypes.bfloat16).astype(np.float64), axis, -1)
    blocks = v.reshape(v.shape[:-1] + (-1, 32))
    amax = np.abs(blocks).max(-1, keepdims=True)
    byte = np.maximum(np.where(amax > 0, np.frexp(amax)[1] - 1 + 127, 0) - down, 1)
    scale = np.exp2(byte - 127.0)
    codes = (blocks / scale).astype(np.float32).astype(dtype).astype(np.float64)
    return np.moveaxis((codes * scale).reshape(v.shape), -1, axis)


WIDE = False


def mx_kscale(k):
    if not WIDE:
        return np.ones(k)
    levels = np.array([10, -10, 5, -5, 0])
    if k % 512:
        return np.exp2(np.random.permutation(np.resize(levels, k // 32))).repeat(32)
    a = np.empty((k // 512, 16))
    for p in range(k // 512):
        a[p, :8] = np.random.permutation(np.resize(levels, 8))
        for g in range(8):
            far = levels[np.abs(levels - a[p, g]) >= 10]
            a[p, g + 8] = far[np.random.randint(len(far))]
    return np.exp2(a.ravel()).repeat(32)


def f64(x):
    return np.asarray(x).astype(np.float64)


def striped(idx):
    return np.tile(idx.reshape(-1, 16).T, (8, 1)).astype(np.uint16)


def unstriped(offs):
    return offs[:16].T.reshape(-1).astype(np.int64)


def striped8(idx):
    return np.concatenate([x.reshape(-1, 16).T for x in idx]).astype(np.uint16)


def runs(offs, k):
    lists = np.stack([offs[16 * r : 16 * r + 16].T.reshape(-1) for r in range(8)]).astype(np.int64)
    return lists[np.arange(k) % 512 // 64]


def pack_weight(w):
    k, n = w.shape
    w = f64(np.asarray(w, np.float32).astype(ml_dtypes.bfloat16)).reshape(k // 32, 32, n)
    amax = np.abs(w).max(1)
    byte = np.clip(np.where(amax > 0, np.frexp(amax)[1] - 1 + 127 - 7, 1), 1, 254)
    scaled = (w * np.exp2(127.0 - byte)[:, None, :]).reshape(k, n).astype(np.float32)
    words = np.ascontiguousarray(scaled.reshape(k // 512, 128, 4, n).transpose(0, 1, 3, 2)).astype(ml_dtypes.float8_e4m3fn).view(np.uint8)
    return words, np.ascontiguousarray(byte.astype(np.uint8).reshape(k // 512, 16, n))


def unpack_weight(words, scales):
    g, p, n, _ = words.shape
    vals = np.ascontiguousarray(words).view(ml_dtypes.float8_e4m3fn).astype(np.float64) * np.repeat(np.exp2(scales.astype(np.float64) - 127.0), 8, axis=1)[..., None]
    return vals.transpose(0, 1, 3, 2).reshape(g * 512, n)


K, T, S, N, H, W = 512, 2048, 256, 512, 512, 128


def setup_inputs():
    n = np.random.standard_normal
    s = mx_kscale(K)[:, None]
    u = mx_kscale(H)
    packed_xT = pack_weight(n((K, T)) * s)
    perm = np.random.permutation(S)
    return {
        "x_words": packed_xT[0],
        "x_scales": packed_xT[1],
        "w1": (n((K, H)) / np.sqrt(K) / s).astype(np.float32),
        "gn": (np.random.uniform(0.5, 1.5, (H, 1)) * u[:, None]).astype(np.float32),
        "w2": (n((H, N)) / np.sqrt(H) / u[:, None]).astype(np.float32),
        "offs": striped(np.random.permutation(T)[:S]),
        "n1": striped(perm[:W]),
        "n2": striped(perm[W:]),
        "n3": striped8(np.stack([np.random.permutation(S) for _ in range(8)])),
        "n4": striped8(np.stack([np.random.permutation(S) for _ in range(8)])),
    }


def reference(x_words, x_scales, w1, gn, w2, offs, n1, n2, n3, n4):
    xq = unpack_weight(x_words, x_scales)[:, unstriped(offs)]
    y = mxq(f64(w1), 0, "e4m3").T @ xq
    pa = y[:, unstriped(n1)]
    pb = y[:, unstriped(n2)]
    rb = pa - pb
    ra = 0.75 * (pa + pb)
    ds = np.zeros((H, S))
    ds[:, unstriped(n1)] = ra
    dt = ds.copy()
    dt[:, unstriped(n2)] = rb
    z = f64(gn) * dt
    h = mxq(f64(w2), 0, "e4m3").T @ mxq(z, 0, "e4m3")
    return np.minimum(np.maximum(h, h[np.arange(N)[:, None], runs(n3, N)]), h[np.arange(N)[:, None], runs(n4, N)])

@@ -1,0 +1,202 @@
+from contextlib import ExitStack
+
+import concourse.mybir as mybir
+
+K, T, S, N, H, W = 512, 2048, 256, 512, 512, 128
+FLOPS = 2 * K * H * S + 2 * H * N * S
+
+F32 = mybir.dt.float32
+BF16 = mybir.dt.bfloat16
+I32 = mybir.dt.int32
+U32 = mybir.dt.uint32
+U16 = mybir.dt.uint16
+U8 = mybir.dt.uint8
+FP8X4 = mybir.dt.float8_e4m3fn_x4
+ALU = mybir.AluOpType
+COPY = mybir.ActivationFunctionType.Copy
+
+P = 128
+PACK = 4
+HALF = 256
+
+
+def tile_picked_layhaarminmx_none_p_kernel(
+    tc, x_words, x_scales, w1, gn, w2, offs, n1, n2, n3, n4, out
+):
+    nc = tc.nc
+    with ExitStack() as ctx:
+        keep = ctx.enter_context(tc.tile_pool(name="keep", bufs=1))
+        psum = ctx.enter_context(tc.psum_pool(name="psum", bufs=1))
+
+        def load_list(src, name):
+            tile = keep.tile(list(src.shape), U16, name=name)
+            nc.sync.dma_start(tile[:], src)
+            return tile
+
+        def load_weight_half(w, u, name):
+            raw = keep.tile([P, PACK, HALF], F32, name=name, tag="w1_raw")
+            nc.sync.dma_start(raw[:], w.rearrange("(p j) c -> p j c", j=PACK)[:, :, u * HALF : (u + 1) * HALF])
+            return raw
+
+        xs = keep.tile([P, T], U8, name="xs")
+        nc.vector.memset(xs[:].bitcast(I32), 0)
+        offs_sb = load_list(offs, "offs_sb")
+        n1_sb = load_list(n1, "n1_sb")
+        n2_sb = load_list(n2, "n2_sb")
+        w1_raw0 = load_weight_half(w1, 0, "w1_raw0")
+        xw = keep.tile([P, T], I32, name="xw", tag="wide")
+        nc.sync.dma_start(xw[:], x_words[0].rearrange("p n t -> p (n t)").bitcast(I32))
+        for q in range(4):
+            nc.scalar.dma_start(xs[32 * q : 32 * q + 4, :].bitcast(I32), x_scales[0, 4 * q : 4 * q + 4, :].bitcast(I32))
+        n3_sb = load_list(n3, "n3_sb")
+        n4_sb = load_list(n4, "n4_sb")
+
+        gain = keep.tile([P, PACK], F32, name="gain")
+        nc.gpsimd.dma_start(gain[:], gn.rearrange("(p t) o -> p (t o)", t=PACK))
+
+        def quantize(values, codes, scales, c0):
+            c1 = c0 + values.shape[1] // PACK
+            nc.vector.quantize_mx(out=codes[:, c0:c1].bitcast(FP8X4), scales=scales[:, c0:c1], in_=values)
+
+        def product(acc, w_codes, w_scales, t, codes, scales, c0, c1):
+            nc.tensor.matmul_mx(
+                out=acc,
+                lhsT=w_codes[:, t * P : (t + 1) * P].bitcast(FP8X4),
+                lhsT_scale=w_scales[:, t * P : (t + 1) * P],
+                rhs=codes[:, c0:c1].bitcast(FP8X4),
+                rhs_scale=scales[:, c0:c1],
+                start=True,
+                stop=True,
+            )
+
+        w1_bf = [keep.tile([P, PACK * HALF], BF16, name=f"w1_bf{u}", align_bytes=64) for u in range(2)]
+        w1_codes = keep.tile([P, H], U32, name="w1_codes", align_bytes=64)
+        w1_scales = keep.tile([P, H], U8, name="w1_scales", align_bytes=64)
+
+        def w1_views(u, raw):
+            dst = w1_bf[u][:].rearrange("p (t m j) -> p m j t", t=PACK, j=PACK)
+            src = raw[:].rearrange("p j (m t) -> p m j t", t=PACK)
+            return dst, src
+
+        def quantize_w1(u, slots):
+            for t0, t1 in slots:
+                c0 = u * P if t0 == 0 else t0 * P + u * 64
+                quantize(w1_bf[u][:, t0 * HALF : t1 * HALF], w1_codes, w1_scales, c0)
+
+        nc.vector.tensor_copy(*w1_views(0, w1_raw0))
+        w1_raw1 = load_weight_half(w1, 1, "w1_raw1")
+        x_sc = keep.tile([P, S], U8, name="x_sc", align_bytes=64)
+        nc.vector.tensor_copy(x_sc[:], xs[:].indirect(offs_sb[:]))
+        quantize_w1(0, [(0, 2), (2, 3), (3, 4)])
+        x_codes = keep.tile([P, S], U32, name="x_codes", align_bytes=64)
+        nc.vector.tensor_copy(x_codes[:], xw[:].bitcast(U32).indirect(offs_sb[:]))
+
+        y = [keep.tile([P, S], F32, name=f"y{t}") for t in range(PACK)]
+        hwin = [keep.tile([P, 2 * S], F32, name=f"hwin{t}") for t in range(PACK)]
+        relay = [keep.tile([P, S], F32, name=f"relay{t}") for t in range(2)]
+        spare = [hwin[t][:, S : 2 * S] for t in range(PACK)]
+        picked = spare[0:2] + [relay[0][:], relay[1][:]]
+        pairs = [relay[0][:], relay[1][:]] + spare[2:4]
+        dt = [keep.tile([P, S], F32, name=f"dt{t}") for t in range(PACK)]
+        moved = [keep.tile([P, S], F32, name=f"moved{t}") for t in range(2)]
+
+        def project(t):
+            acc = psum.tile([P, S], F32, name=f"y_acc{t}", tag=f"bank{t}")
+            product(acc[:], w1_codes, w1_scales, t, x_codes, x_sc, 0, S)
+            nc.vector.tensor_copy(y[t][:], acc[:])
+
+        def fetch_pairs(t):
+            pa, pb = picked[t][:, 0:W], picked[t][:, W:S]
+            nc.scalar.activation(pa, y[t][:].indirect(n1_sb[:]), COPY)
+            nc.scalar.activation(pb, y[t][:].indirect(n2_sb[:]), COPY)
+            nc.vector.tensor_tensor(pairs[t][:, 0:W], pa, pb, ALU.add)
+            nc.vector.tensor_tensor(pairs[t][:, W:S], pa, pb, ALU.subtract)
+
+        def put_sums(t):
+            nc.scalar.activation(dt[t][:].indirect(n1_sb[:]), pairs[t][:, 0:W], COPY, scale=0.75)
+
+        def put_differences(t):
+            nc.scalar.activation(dt[t][:].indirect(n2_sb[:]), pairs[t][:, W:S], COPY)
+
+        def move_halves(u):
+            for t in range(2):
+                nc.sync.dma_start(moved[t][64 * u : 64 * u + 64, :], dt[u][64 * t : 64 * t + 64, :])
+
+        for c0, copy_out in ((0, nc.vector.tensor_copy), (W, nc.scalar.copy)):
+            acc = psum.tile([P, W], F32, name=f"y_acc0_{c0}", tag=f"bank{4 + c0 // W}")
+            product(acc[:], w1_codes, w1_scales, 0, x_codes, x_sc, c0, c0 + W)
+            copy_out(y[0][:, c0 : c0 + W], acc[:])
+        fetch_pairs(0)
+        dst, src = w1_views(1, w1_raw1)
+        nc.vector.tensor_copy(dst[:, :, :, 0:2], src[:, :, :, 0:2])
+        quantize_w1(1, [(0, 2)])
+        project(1)
+        put_sums(0)
+        fetch_pairs(1)
+        nc.vector.tensor_copy(dst[:, :, :, 2:4], src[:, :, :, 2:4])
+        quantize_w1(1, [(2, 3), (3, 4)])
+        project(2)
+        project(3)
+        put_differences(0)
+        move_halves(0)
+        put_sums(1)
+        fetch_pairs(2)
+        put_differences(1)
+        move_halves(1)
+        fetch_pairs(3)
+
+        w2_raw = keep.tile([P, PACK * N], F32, name="w2_raw", tag="wide")
+        nc.sync.dma_start(w2_raw[:], w2.rearrange("(p j) c -> p (j c)", j=PACK))
+        w2_bf = keep.tile([P, PACK * N], BF16, name="w2_bf", tag="staged_bf", align_bytes=64)
+        for u in range(2):
+            dst = w2_bf[:].rearrange("p (t m j) -> p m j t", t=PACK, j=PACK)[:, 64 * u : 64 * u + 64]
+            src = w2_raw[:].rearrange("p (j m t) -> p m j t", t=PACK, j=PACK)[:, 64 * u : 64 * u + 64]
+            nc.vector.tensor_copy(dst, src)
+        w2_codes = keep.tile([P, N], U32, name="w2_codes", align_bytes=64)
+        w2_scales = keep.tile([P, N], U8, name="w2_scales", align_bytes=64)
+        quantize(w2_bf[:], w2_codes, w2_scales, 0)
+
+        z_bf = keep.tile([P, PACK * S], BF16, name="z_bf", tag="staged_bf", align_bytes=64)
+        z_slots = z_bf[:].rearrange("p (j t) -> p t j", t=PACK)
+        dealt = moved + dt[2:]
+
+        def round_z(t, c0, c1):
+            nc.vector.tensor_scalar(z_slots[:, t, c0:c1], dealt[t][:, c0:c1], gain[:, t : t + 1], None, ALU.mult)
+
+        put_sums(2)
+        put_sums(3)
+        put_differences(2)
+        put_differences(3)
+        for t in range(PACK - 1):
+            round_z(t, 0, S)
+        z_codes = keep.tile([P, S], U32, name="z_codes", align_bytes=64)
+        z_scales = keep.tile([P, S], U8, name="z_scales", align_bytes=64)
+        for c0 in (0, W):
+            round_z(PACK - 1, c0, c0 + W)
+        for c0 in (0, W):
+            quantize(z_bf[:, PACK * c0 : PACK * (c0 + W)], z_codes, z_scales, c0)
+
+        out_rows = out.rearrange("(p t) j -> p t j", t=PACK)
+        for t in range(PACK):
+            if t == 0:
+                acc0 = psum.tile([P, W], F32, name="h_acc0a", tag="bank4")
+                acc1 = psum.tile([P, W], F32, name="h_acc0b", tag="bank5")
+                product(acc0[:], w2_codes, w2_scales, t, z_codes, z_scales, 0, W)
+                product(acc1[:], w2_codes, w2_scales, t, z_codes, z_scales, W, S)
+                nc.vector.tensor_copy(hwin[t][:, 0:W], acc0[:])
+                nc.scalar.copy(hwin[t][:, W:S], acc1[:])
+            else:
+                acc = psum.tile([P, S], F32, name=f"h_acc{t}", tag=f"bank{(5 + t) % 8}")
+                product(acc[:], w2_codes, w2_scales, t, z_codes, z_scales, 0, S)
+                nc.vector.tensor_copy(hwin[t][:, 0:S], acc[:])
+            at3 = keep.tile([P, S], F32, name=f"at3_{t}")
+            at4 = keep.tile([P, S], F32, name=f"at4_{t}")
+            nc.scalar.activation(at3[:], hwin[t][:].indirect(n3_sb[:]), COPY)
+            larger = keep.tile([P, S], F32, name=f"larger{t}")
+            nc.vector.tensor_tensor(larger[:], hwin[t][:, 0:S], at3[:], ALU.max)
+            result = keep.tile([P, S], F32, name=f"result{t}")
+            pieces = [(0, S)] if t < PACK - 1 else [(0, W), (W, S)]
+            for c0, c1 in pieces:
+                nc.scalar.activation(at4[:, c0:c1], hwin[t][:].indirect(n4_sb[:, c0 // 16 : c1 // 16]), COPY)
+                nc.vector.tensor_tensor(result[:, c0:c1], larger[:, c0:c1], at4[:, c0:c1], ALU.min)
+                nc.sync.dma_start(out_rows[:, t, c0:c1], result[:, c0:c1])

@@ -17,7 +17,6 @@ COPY = mybir.ActivationFunctionType.Copy
 
 P = 128
 PACK = 4
-HALF = 256
 
 
 def tile_picked_layhaarminmx_none_p_kernel(
@@ -33,26 +32,24 @@ def tile_picked_layhaarminmx_none_p_kernel(
             nc.sync.dma_start(tile[:], src)
             return tile
 
-        def load_weight_half(w, u, name):
-            raw = keep.tile([P, PACK, HALF], F32, name=name, tag="w1_raw")
-            nc.sync.dma_start(raw[:], w.rearrange("(p j) c -> p j c", j=PACK)[:, :, u * HALF : (u + 1) * HALF])
-            return raw
-
         xs = keep.tile([P, T], U8, name="xs")
         nc.vector.memset(xs[:].bitcast(I32), 0)
         offs_sb = load_list(offs, "offs_sb")
         n1_sb = load_list(n1, "n1_sb")
         n2_sb = load_list(n2, "n2_sb")
-        w1_raw0 = load_weight_half(w1, 0, "w1_raw0")
+        w1_raw = keep.tile([P, PACK, H], F32, name="w1_raw")
+        nc.sync.dma_start(w1_raw[:], w1.rearrange("(p j) c -> p j c", j=PACK))
         xw = keep.tile([P, T], I32, name="xw", tag="wide")
         nc.sync.dma_start(xw[:], x_words[0].rearrange("p n t -> p (n t)").bitcast(I32))
-        for q in range(4):
-            nc.scalar.dma_start(xs[32 * q : 32 * q + 4, :].bitcast(I32), x_scales[0, 4 * q : 4 * q + 4, :].bitcast(I32))
         n3_sb = load_list(n3, "n3_sb")
         n4_sb = load_list(n4, "n4_sb")
+        for q in range(4):
+            nc.scalar.dma_start(xs[32 * q : 32 * q + 4, :].bitcast(I32), x_scales[0, 4 * q : 4 * q + 4, :].bitcast(I32))
 
-        gain = keep.tile([P, PACK], F32, name="gain")
-        nc.gpsimd.dma_start(gain[:], gn.rearrange("(p t) o -> p (t o)", t=PACK))
+        gain = keep.tile([P, PACK, 8], F32, name="gain")
+        with nc.allow_non_contiguous_dma(reason="one gain for each partition and slot"):
+            for t in range(PACK):
+                nc.gpsimd.dma_start(gain[:, t, 0:1], gn.rearrange("(b t e) o -> t b e o", t=PACK, e=8)[t])
 
         def quantize(values, codes, scales, c0):
             c1 = c0 + values.shape[1] // PACK
@@ -69,36 +66,26 @@ def tile_picked_layhaarminmx_none_p_kernel(
                 stop=True,
             )
 
-        w1_bf = [keep.tile([P, PACK * HALF], BF16, name=f"w1_bf{u}", align_bytes=64) for u in range(2)]
         w1_codes = keep.tile([P, H], U32, name="w1_codes", align_bytes=64)
         w1_scales = keep.tile([P, H], U8, name="w1_scales", align_bytes=64)
 
-        def w1_views(u, raw):
-            dst = w1_bf[u][:].rearrange("p (t m j) -> p m j t", t=PACK, j=PACK)
-            src = raw[:].rearrange("p j (m t) -> p m j t", t=PACK)
-            return dst, src
-
-        def quantize_w1(u, slots):
-            for t0, t1 in slots:
-                c0 = u * P if t0 == 0 else t0 * P + u * 64
-                quantize(w1_bf[u][:, t0 * HALF : t1 * HALF], w1_codes, w1_scales, c0)
-
-        nc.vector.tensor_copy(*w1_views(0, w1_raw0))
-        w1_raw1 = load_weight_half(w1, 1, "w1_raw1")
+        w1_bf = [keep.tile([P, H], BF16, name=f"w1_bf{t}", align_bytes=64) for t in range(PACK)]
+        src = w1_raw[:].rearrange("p j (b t e i) -> p t b e j i", t=PACK, e=2, i=4)
         x_sc = keep.tile([P, S], U8, name="x_sc", align_bytes=64)
         nc.vector.tensor_copy(x_sc[:], xs[:].indirect(offs_sb[:]))
-        quantize_w1(0, [(0, 2), (2, 3), (3, 4)])
+        for t in range(PACK):
+            round_copy = nc.scalar.copy if t == PACK - 1 else nc.vector.tensor_copy
+            round_copy(w1_bf[t][:].rearrange("p (b e i j) -> p b e j i", e=2, i=4, j=PACK), src[:, t])
+        quantize(w1_bf[0][:], w1_codes, w1_scales, 0)
         x_codes = keep.tile([P, S], U32, name="x_codes", align_bytes=64)
         nc.vector.tensor_copy(x_codes[:], xw[:].bitcast(U32).indirect(offs_sb[:]))
+        for t in range(1, PACK):
+            quantize(w1_bf[t][:], w1_codes, w1_scales, t * P)
 
         y = [keep.tile([P, S], F32, name=f"y{t}") for t in range(PACK)]
         hwin = [keep.tile([P, 2 * S], F32, name=f"hwin{t}") for t in range(PACK)]
-        relay = [keep.tile([P, S], F32, name=f"relay{t}") for t in range(2)]
-        spare = [hwin[t][:, S : 2 * S] for t in range(PACK)]
-        picked = spare[0:2] + [relay[0][:], relay[1][:]]
-        pairs = [relay[0][:], relay[1][:]] + spare[2:4]
+        pairs = [keep.tile([P, S], F32, name=f"pairs{t}") for t in range(PACK)]
         dt = [keep.tile([P, S], F32, name=f"dt{t}") for t in range(PACK)]
-        moved = [keep.tile([P, S], F32, name=f"moved{t}") for t in range(2)]
 
         def project(t):
             acc = psum.tile([P, S], F32, name=f"y_acc{t}", tag=f"bank{t}")
@@ -106,7 +93,7 @@ def tile_picked_layhaarminmx_none_p_kernel(
             nc.vector.tensor_copy(y[t][:], acc[:])
 
         def fetch_pairs(t):
-            pa, pb = picked[t][:, 0:W], picked[t][:, W:S]
+            pa, pb = hwin[t][:, S : S + W], hwin[t][:, S + W : 2 * S]
             nc.scalar.activation(pa, y[t][:].indirect(n1_sb[:]), COPY)
             nc.scalar.activation(pb, y[t][:].indirect(n2_sb[:]), COPY)
             nc.vector.tensor_tensor(pairs[t][:, 0:W], pa, pb, ALU.add)
@@ -118,57 +105,43 @@ def tile_picked_layhaarminmx_none_p_kernel(
         def put_differences(t):
             nc.scalar.activation(dt[t][:].indirect(n2_sb[:]), pairs[t][:, W:S], COPY)
 
-        def move_halves(u):
-            for t in range(2):
-                nc.sync.dma_start(moved[t][64 * u : 64 * u + 64, :], dt[u][64 * t : 64 * t + 64, :])
-
         for c0, copy_out in ((0, nc.vector.tensor_copy), (W, nc.scalar.copy)):
             acc = psum.tile([P, W], F32, name=f"y_acc0_{c0}", tag=f"bank{4 + c0 // W}")
             product(acc[:], w1_codes, w1_scales, 0, x_codes, x_sc, c0, c0 + W)
             copy_out(y[0][:, c0 : c0 + W], acc[:])
         fetch_pairs(0)
-        dst, src = w1_views(1, w1_raw1)
-        nc.vector.tensor_copy(dst[:, :, :, 0:2], src[:, :, :, 0:2])
-        quantize_w1(1, [(0, 2)])
-        project(1)
-        put_sums(0)
-        fetch_pairs(1)
-        nc.vector.tensor_copy(dst[:, :, :, 2:4], src[:, :, :, 2:4])
-        quantize_w1(1, [(2, 3), (3, 4)])
-        project(2)
-        project(3)
-        put_differences(0)
-        move_halves(0)
-        put_sums(1)
-        fetch_pairs(2)
-        put_differences(1)
-        move_halves(1)
-        fetch_pairs(3)
+        for t in range(1, PACK):
+            project(t)
+            fetch_pairs(t)
 
-        w2_raw = keep.tile([P, PACK * N], F32, name="w2_raw", tag="wide")
-        nc.sync.dma_start(w2_raw[:], w2.rearrange("(p j) c -> p (j c)", j=PACK))
+        w2_raw = keep.tile([P, PACK, N], F32, name="w2_raw", tag="wide")
+        w2_rows = w2.rearrange("(b t e) c -> t b e c", t=PACK, e=8)
+        for t in range(PACK):
+            nc.sync.dma_start(w2_raw[:, t, :], w2_rows[t])
         w2_bf = keep.tile([P, PACK * N], BF16, name="w2_bf", tag="staged_bf", align_bytes=64)
-        for u in range(2):
-            dst = w2_bf[:].rearrange("p (t m j) -> p m j t", t=PACK, j=PACK)[:, 64 * u : 64 * u + 64]
-            src = w2_raw[:].rearrange("p (j m t) -> p m j t", t=PACK, j=PACK)[:, 64 * u : 64 * u + 64]
-            nc.vector.tensor_copy(dst, src)
         w2_codes = keep.tile([P, N], U32, name="w2_codes", align_bytes=64)
         w2_scales = keep.tile([P, N], U8, name="w2_scales", align_bytes=64)
-        quantize(w2_bf[:], w2_codes, w2_scales, 0)
+        dst = w2_bf[:].rearrange("p (t g e i j) -> p t g e j i", t=PACK, g=8, i=4, j=PACK)
+        src = w2_raw[:].rearrange("p j (g t e i) -> p t g e j i", t=PACK, g=8, i=4)
+        for t in range(PACK + 1):
+            if t < PACK:
+                nc.vector.tensor_copy(dst[:, t], src[:, t])
+            if t > 0:
+                quantize(w2_bf[:, (t - 1) * N : t * N], w2_codes, w2_scales, (t - 1) * P)
 
         z_bf = keep.tile([P, PACK * S], BF16, name="z_bf", tag="staged_bf", align_bytes=64)
         z_slots = z_bf[:].rearrange("p (j t) -> p t j", t=PACK)
-        dealt = moved + dt[2:]
 
         def round_z(t, c0, c1):
-            nc.vector.tensor_scalar(z_slots[:, t, c0:c1], dealt[t][:, c0:c1], gain[:, t : t + 1], None, ALU.mult)
+            nc.vector.tensor_scalar(z_slots[:, t, c0:c1], dt[t][:, c0:c1], gain[:, t, 0:1], None, ALU.mult)
 
-        put_sums(2)
-        put_sums(3)
-        put_differences(2)
-        put_differences(3)
-        for t in range(PACK - 1):
-            round_z(t, 0, S)
+        for step in range(PACK + 1):
+            if step < PACK:
+                put_sums(step)
+            if step > 0:
+                put_differences(step - 1)
+            if 0 < step < PACK:
+                round_z(step - 1, 0, S)
         z_codes = keep.tile([P, S], U32, name="z_codes", align_bytes=64)
         z_scales = keep.tile([P, S], U8, name="z_scales", align_bytes=64)
         for c0 in (0, W):
@@ -176,7 +149,7 @@ def tile_picked_layhaarminmx_none_p_kernel(
         for c0 in (0, W):
             quantize(z_bf[:, PACK * c0 : PACK * (c0 + W)], z_codes, z_scales, c0)
 
-        out_rows = out.rearrange("(p t) j -> p t j", t=PACK)
+        out_rows = out.rearrange("(g t e) j -> t g e j", t=PACK, e=16)
         for t in range(PACK):
             if t == 0:
                 acc0 = psum.tile([P, W], F32, name="h_acc0a", tag="bank4")
@@ -199,4 +172,4 @@ def tile_picked_layhaarminmx_none_p_kernel(
             for c0, c1 in pieces:
                 nc.scalar.activation(at4[:, c0:c1], hwin[t][:].indirect(n4_sb[:, c0 // 16 : c1 // 16]), COPY)
                 nc.vector.tensor_tensor(result[:, c0:c1], larger[:, c0:c1], at4[:, c0:c1], ALU.min)
-                nc.sync.dma_start(out_rows[:, t, c0:c1], result[:, c0:c1])
+                nc.sync.dma_start(out_rows[t, :, :, c0:c1], result[:, c0:c1])

@@ -32,24 +32,20 @@ def tile_picked_layhaarminmx_none_p_kernel(
             nc.sync.dma_start(tile[:], src)
             return tile
 
-        xs = keep.tile([P, T], U8, name="xs")
+        xs = keep.tile([P, T], U8, name="xs", tag="narrow")
         nc.vector.memset(xs[:].bitcast(I32), 0)
         offs_sb = load_list(offs, "offs_sb")
-        n1_sb = load_list(n1, "n1_sb")
-        n2_sb = load_list(n2, "n2_sb")
         w1_raw = keep.tile([P, PACK, H], F32, name="w1_raw")
         nc.sync.dma_start(w1_raw[:], w1.rearrange("(p j) c -> p j c", j=PACK))
-        xw = keep.tile([P, T], I32, name="xw", tag="wide")
+        xw = keep.tile([P, T], I32, name="xw", tag="wide", align_bytes=64)
         nc.sync.dma_start(xw[:], x_words[0].rearrange("p n t -> p (n t)").bitcast(I32))
+        n1_sb = load_list(n1, "n1_sb")
+        n2_sb = load_list(n2, "n2_sb")
         n3_sb = load_list(n3, "n3_sb")
         n4_sb = load_list(n4, "n4_sb")
-        for q in range(4):
-            nc.scalar.dma_start(xs[32 * q : 32 * q + 4, :].bitcast(I32), x_scales[0, 4 * q : 4 * q + 4, :].bitcast(I32))
-
-        gain = keep.tile([P, PACK, 8], F32, name="gain")
-        with nc.allow_non_contiguous_dma(reason="one gain for each partition and slot"):
-            for t in range(PACK):
-                nc.gpsimd.dma_start(gain[:, t, 0:1], gn.rearrange("(b t e) o -> t b e o", t=PACK, e=8)[t])
+        for r in range(4):
+            queue = nc.gpsimd if r < 2 else nc.scalar
+            queue.dma_start(xs[r:P:32, :].bitcast(I32), x_scales[0, r:16:4, :].bitcast(I32))
 
         def quantize(values, codes, scales, c0):
             c1 = c0 + values.shape[1] // PACK
@@ -69,20 +65,24 @@ def tile_picked_layhaarminmx_none_p_kernel(
         w1_codes = keep.tile([P, H], U32, name="w1_codes", align_bytes=64)
         w1_scales = keep.tile([P, H], U8, name="w1_scales", align_bytes=64)
 
-        w1_bf = [keep.tile([P, H], BF16, name=f"w1_bf{t}", align_bytes=64) for t in range(PACK)]
+        w1_bf = [keep.tile([P, H], BF16, name=f"w1_bf{t}", tag=f"w1_bf{t}", align_bytes=64) for t in range(PACK)]
         src = w1_raw[:].rearrange("p j (b t e i) -> p t b e j i", t=PACK, e=2, i=4)
-        x_sc = keep.tile([P, S], U8, name="x_sc", align_bytes=64)
-        nc.vector.tensor_copy(x_sc[:], xs[:].indirect(offs_sb[:]))
         for t in range(PACK):
             round_copy = nc.scalar.copy if t == PACK - 1 else nc.vector.tensor_copy
             round_copy(w1_bf[t][:].rearrange("p (b e i j) -> p b e j i", e=2, i=4, j=PACK), src[:, t])
-        quantize(w1_bf[0][:], w1_codes, w1_scales, 0)
+        for t in range(PACK):
+            quantize(w1_bf[t][:], w1_codes, w1_scales, t * P)
+        x_sc = keep.tile([P, S], U8, name="x_sc", tag="w1_bf2", align_bytes=64)
+        nc.vector.tensor_copy(x_sc[:], xs[:].indirect(offs_sb[:]))
         x_codes = keep.tile([P, S], U32, name="x_codes", align_bytes=64)
         nc.vector.tensor_copy(x_codes[:], xw[:].bitcast(U32).indirect(offs_sb[:]))
-        for t in range(1, PACK):
-            quantize(w1_bf[t][:], w1_codes, w1_scales, t * P)
 
-        y = [keep.tile([P, S], F32, name=f"y{t}") for t in range(PACK)]
+        gain = keep.tile([P, PACK, 8], F32, name="gain", tag="narrow")
+        with nc.allow_non_contiguous_dma(reason="one gain for each partition and slot"):
+            for t in range(PACK):
+                nc.sync.dma_start(gain[:, t, 0:1], gn.rearrange("(b t e) o -> t b e o", t=PACK, e=8)[t])
+
+        y = [keep.tile([P, S], F32, name=f"y{t}", tag=f"slot{t}", align_bytes=64) for t in range(PACK)]
         hwin = [keep.tile([P, 2 * S], F32, name=f"hwin{t}") for t in range(PACK)]
         pairs = [keep.tile([P, S], F32, name=f"pairs{t}") for t in range(PACK)]
         dt = [keep.tile([P, S], F32, name=f"dt{t}") for t in range(PACK)]
@@ -114,22 +114,21 @@ def tile_picked_layhaarminmx_none_p_kernel(
             project(t)
             fetch_pairs(t)
 
-        w2_raw = keep.tile([P, PACK, N], F32, name="w2_raw", tag="wide")
+        w2_raw = keep.tile([P, PACK, N], F32, name="w2_raw", tag="wide", align_bytes=64)
         w2_rows = w2.rearrange("(b t e) c -> t b e c", t=PACK, e=8)
         for t in range(PACK):
             nc.sync.dma_start(w2_raw[:, t, :], w2_rows[t])
-        w2_bf = keep.tile([P, PACK * N], BF16, name="w2_bf", tag="staged_bf", align_bytes=64)
+        w2_bf = [keep.tile([P, N], BF16, name=f"w2_bf{t}", tag=f"slot{t}", align_bytes=64) for t in range(PACK)]
         w2_codes = keep.tile([P, N], U32, name="w2_codes", align_bytes=64)
         w2_scales = keep.tile([P, N], U8, name="w2_scales", align_bytes=64)
-        dst = w2_bf[:].rearrange("p (t g e i j) -> p t g e j i", t=PACK, g=8, i=4, j=PACK)
-        src = w2_raw[:].rearrange("p j (g t e i) -> p t g e j i", t=PACK, g=8, i=4)
+        src = w2_raw[:].rearrange("p j (b t e i) -> p t b e j i", t=PACK, e=2, i=4)
         for t in range(PACK + 1):
             if t < PACK:
-                nc.vector.tensor_copy(dst[:, t], src[:, t])
+                nc.vector.tensor_copy(w2_bf[t][:].rearrange("p (b e i j) -> p b e j i", e=2, i=4, j=PACK), src[:, t])
             if t > 0:
-                quantize(w2_bf[:, (t - 1) * N : t * N], w2_codes, w2_scales, (t - 1) * P)
+                quantize(w2_bf[t - 1][:], w2_codes, w2_scales, (t - 1) * P)
 
-        z_bf = keep.tile([P, PACK * S], BF16, name="z_bf", tag="staged_bf", align_bytes=64)
+        z_bf = keep.tile([P, PACK * S], BF16, name="z_bf", tag="wide", align_bytes=64)
         z_slots = z_bf[:].rearrange("p (j t) -> p t j", t=PACK)
 
         def round_z(t, c0, c1):
@@ -149,7 +148,7 @@ def tile_picked_layhaarminmx_none_p_kernel(
         for c0 in (0, W):
             quantize(z_bf[:, PACK * c0 : PACK * (c0 + W)], z_codes, z_scales, c0)
 
-        out_rows = out.rearrange("(g t e) j -> t g e j", t=PACK, e=16)
+        out_rows = out.rearrange("(b t e) j -> t b e j", t=PACK, e=8)
         for t in range(PACK):
             if t == 0:
                 acc0 = psum.tile([P, W], F32, name="h_acc0a", tag="bank4")

@@ -17,6 +17,8 @@ COPY = mybir.ActivationFunctionType.Copy
 
 P = 128
 PACK = 4
+HALF = 256
+LOW, HIGH, ALL = slice(0, 64), slice(64, 128), slice(0, 128)
 
 
 def tile_picked_layhaarminmx_none_p_kernel(
@@ -25,6 +27,7 @@ def tile_picked_layhaarminmx_none_p_kernel(
     nc = tc.nc
     with ExitStack() as ctx:
         keep = ctx.enter_context(tc.tile_pool(name="keep", bufs=1))
+        shared = ctx.enter_context(tc.tile_pool(name="shared", bufs=1))
         psum = ctx.enter_context(tc.psum_pool(name="psum", bufs=1))
 
         def load_list(src, name):
@@ -35,17 +38,18 @@ def tile_picked_layhaarminmx_none_p_kernel(
         xs = keep.tile([P, T], U8, name="xs", tag="narrow")
         nc.vector.memset(xs[:].bitcast(I32), 0)
         offs_sb = load_list(offs, "offs_sb")
-        w1_raw = keep.tile([P, PACK, H], F32, name="w1_raw")
-        nc.sync.dma_start(w1_raw[:], w1.rearrange("(p j) c -> p j c", j=PACK))
-        xw = keep.tile([P, T], I32, name="xw", tag="wide", align_bytes=64)
-        nc.sync.dma_start(xw[:], x_words[0].rearrange("p n t -> p (n t)").bitcast(I32))
         n1_sb = load_list(n1, "n1_sb")
         n2_sb = load_list(n2, "n2_sb")
         n3_sb = load_list(n3, "n3_sb")
+        w1_rows = w1.rearrange("(p j) c -> p j c", j=PACK)
+        w1_raw = [keep.tile([P, PACK, HALF], F32, name=f"w1_raw{u}", tag=f"w1_raw{u}") for u in range(2)]
+        nc.sync.dma_start(w1_raw[0][:], w1_rows[:, :, 0:HALF])
+        xw = keep.tile([P, T], I32, name="xw", tag="wide", align_bytes=64)
+        nc.sync.dma_start(xw[:], x_words[0].rearrange("p n t -> p (n t)").bitcast(I32))
+        nc.sync.dma_start(w1_raw[1][:], w1_rows[:, :, HALF:H])
         n4_sb = load_list(n4, "n4_sb")
         for r in range(4):
-            queue = nc.gpsimd if r < 2 else nc.scalar
-            queue.dma_start(xs[r:P:32, :].bitcast(I32), x_scales[0, r:16:4, :].bitcast(I32))
+            nc.scalar.dma_start(xs[r:P:32, :].bitcast(I32), x_scales[0, r:16:4, :].bitcast(I32))
 
         def quantize(values, codes, scales, c0):
             c1 = c0 + values.shape[1] // PACK
@@ -65,14 +69,27 @@ def tile_picked_layhaarminmx_none_p_kernel(
         w1_codes = keep.tile([P, H], U32, name="w1_codes", align_bytes=64)
         w1_scales = keep.tile([P, H], U8, name="w1_scales", align_bytes=64)
 
-        w1_bf = [keep.tile([P, H], BF16, name=f"w1_bf{t}", tag=f"w1_bf{t}", align_bytes=64) for t in range(PACK)]
-        src = w1_raw[:].rearrange("p j (b t e i) -> p t b e j i", t=PACK, e=2, i=4)
-        for t in range(PACK):
-            round_copy = nc.scalar.copy if t == PACK - 1 else nc.vector.tensor_copy
-            round_copy(w1_bf[t][:].rearrange("p (b e i j) -> p b e j i", e=2, i=4, j=PACK), src[:, t])
-        for t in range(PACK):
-            quantize(w1_bf[t][:], w1_codes, w1_scales, t * P)
-        x_sc = keep.tile([P, S], U8, name="x_sc", tag="w1_bf2", align_bytes=64)
+        w1_column = {(0, 0): 0, (0, 1): 64, (1, 1): 128, (1, 0): 192, (0, 2): 256, (1, 2): 320, (0, 3): 384, (1, 3): 448}
+
+        def round_w1(u, slots):
+            src = w1_raw[u][:].rearrange("p j (b t e i) -> p t b e j i", t=PACK, e=2, i=4)
+            staged = []
+            for t in slots:
+                bf = keep.tile([P, HALF], BF16, name=f"w1_bf{u}{t}", tag=f"w1_bf{u}{t}", align_bytes=64)
+                if (u, t) == (0, 0):
+                    rows = w1_raw[u][:].rearrange("p j (b t e) -> p t b e j", t=PACK, e=8)
+                    nc.scalar.activation(bf[:].rearrange("p (b e j) -> p b e j", e=8, j=PACK), rows[:, t], COPY)
+                else:
+                    nc.vector.tensor_copy(bf[:].rearrange("p (b e i j) -> p b e j i", e=2, i=4, j=PACK), src[:, t])
+                staged.append((t, bf))
+            return staged
+
+        def quantize_w1(u, staged):
+            for t, bf in staged:
+                quantize(bf[:], w1_codes, w1_scales, w1_column[(u, t)])
+
+        quantize_w1(0, round_w1(0, [1, 2, 3, 0]))
+        x_sc = keep.tile([P, S], U8, name="x_sc", tag="w1_bf03", align_bytes=64)
         nc.vector.tensor_copy(x_sc[:], xs[:].indirect(offs_sb[:]))
         x_codes = keep.tile([P, S], U32, name="x_codes", align_bytes=64)
         nc.vector.tensor_copy(x_codes[:], xw[:].bitcast(U32).indirect(offs_sb[:]))
@@ -82,9 +99,13 @@ def tile_picked_layhaarminmx_none_p_kernel(
             for t in range(PACK):
                 nc.sync.dma_start(gain[:, t, 0:1], gn.rearrange("(b t e) o -> t b e o", t=PACK, e=8)[t])
 
-        y = [keep.tile([P, S], F32, name=f"y{t}", tag=f"slot{t}", align_bytes=64) for t in range(PACK)]
+        y = [shared.tile([P, S], F32, name=f"y{t}", offset=4 * S * t, align_bytes=64) for t in range(PACK)]
+        w2_raw = keep.tile([P, PACK, N], F32, name="w2_raw", tag="wide", align_bytes=64)
+        w2_rows = w2.rearrange("(b t e) c -> t b e c", t=PACK, e=8)
+        for t in range(PACK):
+            nc.sync.dma_start(w2_raw[:, t, :], w2_rows[t])
         hwin = [keep.tile([P, 2 * S], F32, name=f"hwin{t}") for t in range(PACK)]
-        pairs = [keep.tile([P, S], F32, name=f"pairs{t}") for t in range(PACK)]
+        pairs = [None] + [keep.tile([P, S], F32, name=f"pairs{t}") for t in range(1, PACK)]
         dt = [keep.tile([P, S], F32, name=f"dt{t}") for t in range(PACK)]
 
         def project(t):
@@ -109,42 +130,54 @@ def tile_picked_layhaarminmx_none_p_kernel(
             acc = psum.tile([P, W], F32, name=f"y_acc0_{c0}", tag=f"bank{4 + c0 // W}")
             product(acc[:], w1_codes, w1_scales, 0, x_codes, x_sc, c0, c0 + W)
             copy_out(y[0][:, c0 : c0 + W], acc[:])
+        moved = keep.tile([P, S], F32, name="moved")
+        quantize_w1(1, round_w1(1, [1, 0]))
+        later = round_w1(1, [2, 3])
+        pairs[0] = keep.tile([P, S], F32, name="pairs0", tag="w1_raw1")
         fetch_pairs(0)
-        for t in range(1, PACK):
-            project(t)
-            fetch_pairs(t)
+        project(1)
+        put_sums(0)
+        fetch_pairs(1)
+        quantize_w1(1, later)
+        project(2)
+        project(3)
+        put_differences(0)
+        nc.sync.dma_start(moved[LOW, :], dt[0][HIGH, :])
+        put_sums(1)
+        fetch_pairs(2)
+        put_differences(1)
+        nc.sync.dma_start(moved[HIGH, :], dt[1][LOW, :])
+        fetch_pairs(3)
 
-        w2_raw = keep.tile([P, PACK, N], F32, name="w2_raw", tag="wide", align_bytes=64)
-        w2_rows = w2.rearrange("(b t e) c -> t b e c", t=PACK, e=8)
-        for t in range(PACK):
-            nc.sync.dma_start(w2_raw[:, t, :], w2_rows[t])
-        w2_bf = [keep.tile([P, N], BF16, name=f"w2_bf{t}", tag=f"slot{t}", align_bytes=64) for t in range(PACK)]
+        w2_all = shared.tile([P, PACK, N], BF16, name="w2_bf", offset=0, align_bytes=64)
+        w2_bf = [w2_all[:, t, :] for t in range(PACK)]
         w2_codes = keep.tile([P, N], U32, name="w2_codes", align_bytes=64)
         w2_scales = keep.tile([P, N], U8, name="w2_scales", align_bytes=64)
         src = w2_raw[:].rearrange("p j (b t e i) -> p t b e j i", t=PACK, e=2, i=4)
         for t in range(PACK + 1):
             if t < PACK:
-                nc.vector.tensor_copy(w2_bf[t][:].rearrange("p (b e i j) -> p b e j i", e=2, i=4, j=PACK), src[:, t])
+                nc.vector.tensor_copy(w2_bf[t].rearrange("p (b e i j) -> p b e j i", e=2, i=4, j=PACK), src[:, t])
             if t > 0:
-                quantize(w2_bf[t - 1][:], w2_codes, w2_scales, (t - 1) * P)
+                quantize(w2_bf[t - 1], w2_codes, w2_scales, (t - 1) * P)
 
         z_bf = keep.tile([P, PACK * S], BF16, name="z_bf", tag="wide", align_bytes=64)
         z_slots = z_bf[:].rearrange("p (j t) -> p t j", t=PACK)
 
-        def round_z(t, c0, c1):
-            nc.vector.tensor_scalar(z_slots[:, t, c0:c1], dt[t][:, c0:c1], gain[:, t, 0:1], None, ALU.mult)
+        def round_z(t, values, rows, c0, c1):
+            nc.vector.tensor_scalar(z_slots[rows, t, c0:c1], values[rows, c0:c1], gain[rows, t, 0:1], None, ALU.mult)
 
-        for step in range(PACK + 1):
-            if step < PACK:
-                put_sums(step)
-            if step > 0:
-                put_differences(step - 1)
-            if 0 < step < PACK:
-                round_z(step - 1, 0, S)
+        put_sums(2)
+        put_sums(3)
+        put_differences(2)
+        put_differences(3)
+        round_z(0, dt[0], LOW, 0, S)
+        round_z(0, dt[1], HIGH, 0, S)
+        round_z(1, moved, ALL, 0, S)
+        round_z(2, dt[2], ALL, 0, S)
         z_codes = keep.tile([P, S], U32, name="z_codes", align_bytes=64)
         z_scales = keep.tile([P, S], U8, name="z_scales", align_bytes=64)
         for c0 in (0, W):
-            round_z(PACK - 1, c0, c0 + W)
+            round_z(3, dt[3], ALL, c0, c0 + W)
         for c0 in (0, W):
             quantize(z_bf[:, PACK * c0 : PACK * (c0 + W)], z_codes, z_scales, c0)
 

from contextlib import ExitStack

import concourse.mybir as mybir

K, T, S, N, H, W = 512, 2048, 256, 512, 512, 128
FLOPS = 2 * K * H * S + 2 * H * N * S

F32 = mybir.dt.float32
BF16 = mybir.dt.bfloat16
I32 = mybir.dt.int32
U32 = mybir.dt.uint32
U16 = mybir.dt.uint16
U8 = mybir.dt.uint8
FP8X4 = mybir.dt.float8_e4m3fn_x4
ALU = mybir.AluOpType
COPY = mybir.ActivationFunctionType.Copy

P = 128
PACK = 4
HALF = 256
LOW, HIGH, ALL = slice(0, 64), slice(64, 128), slice(0, 128)


def tile_picked_layhaarminmx_none_p_kernel(
    tc, x_words, x_scales, w1, gn, w2, offs, n1, n2, n3, n4, out
):
    nc = tc.nc
    with ExitStack() as ctx:
        keep = ctx.enter_context(tc.tile_pool(name="keep", bufs=1))
        shared = ctx.enter_context(tc.tile_pool(name="shared", bufs=1))
        psum = ctx.enter_context(tc.psum_pool(name="psum", bufs=1))

        def load_list(src, name):
            tile = keep.tile(list(src.shape), U16, name=name)
            nc.sync.dma_start(tile[:], src)
            return tile

        xs = keep.tile([P, T], U8, name="xs", tag="narrow")
        nc.vector.memset(xs[:].bitcast(I32), 0)
        offs_sb = load_list(offs, "offs_sb")
        n1_sb = load_list(n1, "n1_sb")
        n2_sb = load_list(n2, "n2_sb")
        n3_sb = load_list(n3, "n3_sb")
        w1_rows = w1.rearrange("(p j) c -> p j c", j=PACK)
        w1_raw = [keep.tile([P, PACK, HALF], F32, name=f"w1_raw{u}", tag=f"w1_raw{u}") for u in range(2)]
        nc.sync.dma_start(w1_raw[0][:], w1_rows[:, :, 0:HALF])
        xw = keep.tile([P, T], I32, name="xw", tag="wide", align_bytes=64)
        nc.sync.dma_start(xw[:], x_words[0].rearrange("p n t -> p (n t)").bitcast(I32))
        nc.sync.dma_start(w1_raw[1][:], w1_rows[:, :, HALF:H])
        n4_sb = load_list(n4, "n4_sb")
        for r in range(4):
            nc.scalar.dma_start(xs[r:P:32, :].bitcast(I32), x_scales[0, r:16:4, :].bitcast(I32))

        def quantize(values, codes, scales, c0):
            c1 = c0 + values.shape[1] // PACK
            nc.vector.quantize_mx(out=codes[:, c0:c1].bitcast(FP8X4), scales=scales[:, c0:c1], in_=values)

        def product(acc, w_codes, w_scales, t, codes, scales, c0, c1):
            nc.tensor.matmul_mx(
                out=acc,
                lhsT=w_codes[:, t * P : (t + 1) * P].bitcast(FP8X4),
                lhsT_scale=w_scales[:, t * P : (t + 1) * P],
                rhs=codes[:, c0:c1].bitcast(FP8X4),
                rhs_scale=scales[:, c0:c1],
                start=True,
                stop=True,
            )

        w1_codes = keep.tile([P, H], U32, name="w1_codes", align_bytes=64)
        w1_scales = keep.tile([P, H], U8, name="w1_scales", align_bytes=64)

        w1_column = {(0, 0): 0, (0, 1): 64, (1, 1): 128, (1, 0): 192, (0, 2): 256, (1, 2): 320, (0, 3): 384, (1, 3): 448}

        def round_w1(u, slots):
            src = w1_raw[u][:].rearrange("p j (b t e i) -> p t b e j i", t=PACK, e=2, i=4)
            staged = []
            for t in slots:
                bf = keep.tile([P, HALF], BF16, name=f"w1_bf{u}{t}", tag=f"w1_bf{u}{t}", align_bytes=64)
                if (u, t) == (0, 0):
                    rows = w1_raw[u][:].rearrange("p j (b t e) -> p t b e j", t=PACK, e=8)
                    nc.scalar.activation(bf[:].rearrange("p (b e j) -> p b e j", e=8, j=PACK), rows[:, t], COPY)
                else:
                    nc.vector.tensor_copy(bf[:].rearrange("p (b e i j) -> p b e j i", e=2, i=4, j=PACK), src[:, t])
                staged.append((t, bf))
            return staged

        def quantize_w1(u, staged):
            for t, bf in staged:
                quantize(bf[:], w1_codes, w1_scales, w1_column[(u, t)])

        quantize_w1(0, round_w1(0, [1, 2, 3, 0]))
        x_sc = keep.tile([P, S], U8, name="x_sc", tag="w1_bf03", align_bytes=64)
        nc.vector.tensor_copy(x_sc[:], xs[:].indirect(offs_sb[:]))
        x_codes = keep.tile([P, S], U32, name="x_codes", align_bytes=64)
        nc.vector.tensor_copy(x_codes[:], xw[:].bitcast(U32).indirect(offs_sb[:]))

        gain = keep.tile([P, PACK, 8], F32, name="gain", tag="narrow")
        with nc.allow_non_contiguous_dma(reason="one gain for each partition and slot"):
            for t in range(PACK):
                nc.sync.dma_start(gain[:, t, 0:1], gn.rearrange("(b t e) o -> t b e o", t=PACK, e=8)[t])

        y = [shared.tile([P, S], F32, name=f"y{t}", offset=4 * S * t, align_bytes=64) for t in range(PACK)]
        w2_raw = keep.tile([P, PACK, N], F32, name="w2_raw", tag="wide", align_bytes=64)
        w2_rows = w2.rearrange("(b t e) c -> t b e c", t=PACK, e=8)
        for t in range(PACK):
            nc.sync.dma_start(w2_raw[:, t, :], w2_rows[t])
        hwin = [keep.tile([P, 2 * S], F32, name=f"hwin{t}") for t in range(PACK)]
        pairs = [None] + [keep.tile([P, S], F32, name=f"pairs{t}") for t in range(1, PACK)]
        dt = [keep.tile([P, S], F32, name=f"dt{t}") for t in range(PACK)]

        def project(t):
            acc = psum.tile([P, S], F32, name=f"y_acc{t}", tag=f"bank{t}")
            product(acc[:], w1_codes, w1_scales, t, x_codes, x_sc, 0, S)
            nc.vector.tensor_copy(y[t][:], acc[:])

        def fetch_pairs(t):
            pa, pb = hwin[t][:, S : S + W], hwin[t][:, S + W : 2 * S]
            nc.scalar.activation(pa, y[t][:].indirect(n1_sb[:]), COPY)
            nc.scalar.activation(pb, y[t][:].indirect(n2_sb[:]), COPY)
            nc.vector.tensor_tensor(pairs[t][:, 0:W], pa, pb, ALU.add)
            nc.vector.tensor_tensor(pairs[t][:, W:S], pa, pb, ALU.subtract)

        def put_sums(t):
            nc.scalar.activation(dt[t][:].indirect(n1_sb[:]), pairs[t][:, 0:W], COPY, scale=0.75)

        def put_differences(t):
            nc.scalar.activation(dt[t][:].indirect(n2_sb[:]), pairs[t][:, W:S], COPY)

        for c0, copy_out in ((0, nc.vector.tensor_copy), (W, nc.scalar.copy)):
            acc = psum.tile([P, W], F32, name=f"y_acc0_{c0}", tag=f"bank{4 + c0 // W}")
            product(acc[:], w1_codes, w1_scales, 0, x_codes, x_sc, c0, c0 + W)
            copy_out(y[0][:, c0 : c0 + W], acc[:])
        moved = keep.tile([P, S], F32, name="moved")
        quantize_w1(1, round_w1(1, [1, 0]))
        later = round_w1(1, [2, 3])
        pairs[0] = keep.tile([P, S], F32, name="pairs0", tag="w1_raw1")
        fetch_pairs(0)
        project(1)
        put_sums(0)
        fetch_pairs(1)
        quantize_w1(1, later)
        project(2)
        project(3)
        put_differences(0)
        nc.sync.dma_start(moved[LOW, :], dt[0][HIGH, :])
        put_sums(1)
        fetch_pairs(2)
        put_differences(1)
        nc.sync.dma_start(moved[HIGH, :], dt[1][LOW, :])
        fetch_pairs(3)

        w2_all = shared.tile([P, PACK, N], BF16, name="w2_bf", offset=0, align_bytes=64)
        w2_bf = [w2_all[:, t, :] for t in range(PACK)]
        w2_codes = keep.tile([P, N], U32, name="w2_codes", align_bytes=64)
        w2_scales = keep.tile([P, N], U8, name="w2_scales", align_bytes=64)
        src = w2_raw[:].rearrange("p j (b t e i) -> p t b e j i", t=PACK, e=2, i=4)
        for t in range(PACK + 1):
            if t < PACK:
                nc.vector.tensor_copy(w2_bf[t].rearrange("p (b e i j) -> p b e j i", e=2, i=4, j=PACK), src[:, t])
            if t > 0:
                quantize(w2_bf[t - 1], w2_codes, w2_scales, (t - 1) * P)

        z_bf = keep.tile([P, PACK * S], BF16, name="z_bf", tag="wide", align_bytes=64)
        z_slots = z_bf[:].rearrange("p (j t) -> p t j", t=PACK)

        def round_z(t, values, rows, c0, c1):
            nc.vector.tensor_scalar(z_slots[rows, t, c0:c1], values[rows, c0:c1], gain[rows, t, 0:1], None, ALU.mult)

        put_sums(2)
        put_sums(3)
        put_differences(2)
        put_differences(3)
        round_z(0, dt[0], LOW, 0, S)
        round_z(0, dt[1], HIGH, 0, S)
        round_z(1, moved, ALL, 0, S)
        round_z(2, dt[2], ALL, 0, S)
        z_codes = keep.tile([P, S], U32, name="z_codes", align_bytes=64)
        z_scales = keep.tile([P, S], U8, name="z_scales", align_bytes=64)
        for c0 in (0, W):
            round_z(3, dt[3], ALL, c0, c0 + W)
        for c0 in (0, W):
            quantize(z_bf[:, PACK * c0 : PACK * (c0 + W)], z_codes, z_scales, c0)

        out_rows = out.rearrange("(b t e) j -> t b e j", t=PACK, e=8)
        for t in range(PACK):
            if t == 0:
                acc0 = psum.tile([P, W], F32, name="h_acc0a", tag="bank4")
                acc1 = psum.tile([P, W], F32, name="h_acc0b", tag="bank5")
                product(acc0[:], w2_codes, w2_scales, t, z_codes, z_scales, 0, W)
                product(acc1[:], w2_codes, w2_scales, t, z_codes, z_scales, W, S)
                nc.vector.tensor_copy(hwin[t][:, 0:W], acc0[:])
                nc.scalar.copy(hwin[t][:, W:S], acc1[:])
            else:
                acc = psum.tile([P, S], F32, name=f"h_acc{t}", tag=f"bank{(5 + t) % 8}")
                product(acc[:], w2_codes, w2_scales, t, z_codes, z_scales, 0, S)
                nc.vector.tensor_copy(hwin[t][:, 0:S], acc[:])
            at3 = keep.tile([P, S], F32, name=f"at3_{t}")
            at4 = keep.tile([P, S], F32, name=f"at4_{t}")
            nc.scalar.activation(at3[:], hwin[t][:].indirect(n3_sb[:]), COPY)
            larger = keep.tile([P, S], F32, name=f"larger{t}")
            nc.vector.tensor_tensor(larger[:], hwin[t][:, 0:S], at3[:], ALU.max)
            result = keep.tile([P, S], F32, name=f"result{t}")
            pieces = [(0, S)] if t < PACK - 1 else [(0, W), (W, S)]
            for c0, c1 in pieces:
                nc.scalar.activation(at4[:, c0:c1], hwin[t][:].indirect(n4_sb[:, c0 // 16 : c1 // 16]), COPY)
                nc.vector.tensor_tensor(result[:, c0:c1], larger[:, c0:c1], at4[:, c0:c1], ALU.min)
                nc.sync.dma_start(out_rows[t, :, :, c0:c1], result[:, c0:c1])
